import numpy as np
import ml_dtypes


def mxq(x, axis, fmt="e4m3"):
    dtype, down = {"e4m3": (ml_dtypes.float8_e4m3fn, 7), "e5m2": (ml_dtypes.float8_e5m2, 14)}[fmt]
    v = np.moveaxis(np.asarray(x, np.float32).astype(ml_dtypes.bfloat16).astype(np.float64), axis, -1)
    blocks = v.reshape(v.shape[:-1] + (-1, 32))
    amax = np.abs(blocks).max(-1, keepdims=True)
    byte = np.maximum(np.where(amax > 0, np.frexp(amax)[1] - 1 + 127, 0) - down, 1)
    scale = np.exp2(byte - 127.0)
    codes = (blocks / scale).astype(np.float32).astype(dtype).astype(np.float64)
    return np.moveaxis((codes * scale).reshape(v.shape), -1, axis)


WIDE = False


def mx_kscale(k):
    if not WIDE:
        return np.ones(k)
    levels = np.array([10, -10, 5, -5, 0])
    if k % 512:
        return np.exp2(np.random.permutation(np.resize(levels, k // 32))).repeat(32)
    a = np.empty((k // 512, 16))
    for p in range(k // 512):
        a[p, :8] = np.random.permutation(np.resize(levels, 8))
        for g in range(8):
            far = levels[np.abs(levels - a[p, g]) >= 10]
            a[p, g + 8] = far[np.random.randint(len(far))]
    return np.exp2(a.ravel()).repeat(32)


def f64(x):
    return np.asarray(x).astype(np.float64)


def striped(idx):
    return np.tile(idx.reshape(-1, 16).T, (8, 1)).astype(np.uint16)


def unstriped(offs):
    return offs[:16].T.reshape(-1).astype(np.int64)


def pack_weight(w):
    k, n = w.shape
    w = f64(np.asarray(w, np.float32).astype(ml_dtypes.bfloat16)).reshape(k // 32, 32, n)
    amax = np.abs(w).max(1)
    byte = np.clip(np.where(amax > 0, np.frexp(amax)[1] - 1 + 127 - 7, 1), 1, 254)
    scaled = (w * np.exp2(127.0 - byte)[:, None, :]).reshape(k, n).astype(np.float32)
    words = np.ascontiguousarray(scaled.reshape(k // 512, 128, 4, n).transpose(0, 1, 3, 2)).astype(ml_dtypes.float8_e4m3fn).view(np.uint8)
    return words, np.ascontiguousarray(byte.astype(np.uint8).reshape(k // 512, 16, n))


def unpack_weight(words, scales):
    g, p, n, _ = words.shape
    vals = np.ascontiguousarray(words).view(ml_dtypes.float8_e4m3fn).astype(np.float64) * np.repeat(np.exp2(scales.astype(np.float64) - 127.0), 8, axis=1)[..., None]
    return vals.transpose(0, 1, 3, 2).reshape(g * 512, n)


K, T, S, N, H, U = 1024, 2048, 512, 128, 512, 1024


def setup_inputs():
    n = np.random.standard_normal
    s = mx_kscale(K)[:, None]
    u = mx_kscale(H)
    packed_xT = pack_weight(n((K, T)) * s)
    return {
        "x_words": packed_xT[0],
        "x_scales": packed_xT[1],
        "w1": (n((K, H)) / np.sqrt(K) / s).astype(np.float32),
        "w2": (n((K, H)) / np.sqrt(K) / s).astype(np.float32),
        "unit": (np.random.uniform(0.6, 1.4, (H, 1)) * u[:, None]).astype(np.float32),
        "w3": (n((H, N)) / np.sqrt(H) / u[:, None]).astype(np.float32),
        "offs": striped(np.random.permutation(T)[:S]),
        "b1": striped(np.random.permutation(np.concatenate([np.arange(S), np.random.randint(0, S, U - S)]))),
        "b2": striped(np.random.permutation(np.concatenate([np.arange(S), np.random.randint(0, S, U - S)]))),
        "usr": striped(np.random.permutation(np.concatenate([np.arange(S), np.random.randint(0, S, U - S)]))),
    }


def reference(x_words, x_scales, w1, w2, unit, w3, offs, b1, b2, usr):
    xq = unpack_weight(x_words, x_scales)[:, unstriped(offs)]
    y = mxq(f64(w1), 0, "e4m3").T @ xq
    y_1 = y[:, unstriped(b1)]
    z1 = mxq(f64(w2), 0, "e4m3").T @ xq
    z_1 = z1[:, unstriped(b1)]
    v1_ = y_1 * z_1
    y_2 = y[:, unstriped(b2)]
    z_2 = z1[:, unstriped(b2)]
    v2_ = y_2 * z_2
    zu = z1[:, unstriped(usr)]
    hid = f64(unit) * (np.maximum(v1_, v2_) - (0.6 * np.minimum(v1_, v2_)) + zu)
    return mxq(f64(w3), 0, "e4m3").T @ mxq(hid, 0, "e4m3")

@@ -1,0 +1,226 @@
+from contextlib import ExitStack
+
+import concourse.mybir as mybir
+
+K, T, S, N, H, U = 1024, 2048, 512, 128, 512, 1024
+FLOPS = 2 * (2 * K * H * S + H * N * U)
+
+F32 = mybir.dt.float32
+BF16 = mybir.dt.bfloat16
+I32 = mybir.dt.int32
+U32 = mybir.dt.uint32
+U16 = mybir.dt.uint16
+U8 = mybir.dt.uint8
+FP8X4 = mybir.dt.float8_e4m3fn_x4
+ALU = mybir.AluOpType
+COPY = mybir.ActivationFunctionType.Copy
+
+P = 128
+PACK = 4
+K_PASS = P * PACK
+PASSES = K // K_PASS
+CHUNKS = (384, 384, 256)
+FUSED = ((0, 1), (), (0,))
+
+
+def tile_picked_ycompet_sec_p_kernel(tc, x_words, x_scales, w1, w2, unit, w3, offs, b1, b2, usr, out):
+    nc = tc.nc
+    with ExitStack() as ctx:
+        lists = ctx.enter_context(tc.tile_pool(name="lists", bufs=1))
+        keep = ctx.enter_context(tc.tile_pool(name="keep", bufs=1))
+        psum = ctx.enter_context(tc.psum_pool(name="psum", bufs=1))
+
+        def load_list(src, name):
+            tile = lists.tile(list(src.shape), U16, name=name)
+            nc.sync.dma_start(tile[:], src)
+            return tile
+
+        def load_words(o):
+            tile = keep.tile([P, T], I32, name="x_table%d" % o)
+            nc.sync.dma_start(tile[:], x_words[o].rearrange("p n r -> p (n r)").bitcast(I32))
+            return tile
+
+        def load_weight(w, o, parts, name):
+            width = w.shape[1] // parts
+            tiles = []
+            for h in range(parts):
+                tile = keep.tile([P, PACK, width], F32, name="%s_raw%d_%d" % (name, o, h))
+                rows = w[o * K_PASS : (o + 1) * K_PASS, h * width : (h + 1) * width]
+                nc.sync.dma_start(tile[:], rows.rearrange("(p j) c -> p j c", j=PACK))
+                tiles.append(tile)
+            return tiles
+
+        scale_table = keep.tile([P, T], U8, name="scale_table")
+        nc.vector.memset(scale_table[:].bitcast(I32), 0)
+        for q in range(4):
+            nc.scalar.dma_start(
+                scale_table[32 * q : 32 * q + 4 * PASSES, :].bitcast(I32),
+                x_scales[:, 4 * q : 4 * q + 4, :].bitcast(I32),
+            )
+
+        x_table = [None] * PASSES
+        w2_raw = [load_weight(w2, 0, 1, "w2")]
+        offs_sb = load_list(offs, "offs_sb")
+        x_table[0] = load_words(0)
+        w2_raw.append(load_weight(w2, 1, 1, "w2"))
+        x_table[1] = load_words(1)
+        unit_sb = keep.tile([P, PACK], F32, name="unit_sb")
+        nc.sync.dma_start(unit_sb[:], unit.rearrange("(p t) one -> p (t one)", t=PACK))
+        usr_sb = load_list(usr, "usr_sb")
+        w1_raw = [load_weight(w1, 0, 2, "w1"), load_weight(w1, 1, 2, "w1")]
+        b1_sb = load_list(b1, "b1_sb")
+        b2_sb = load_list(b2, "b2_sb")
+        w3_raw = load_weight(w3, 0, 1, "w3")[0]
+
+        def gather_words(o):
+            tile = keep.tile([P, S], U32, name="x_codes%d" % o, align_bytes=64)
+            nc.vector.tensor_copy(tile[:], x_table[o][:].bitcast(U32).indirect(offs_sb[:]))
+            return tile
+
+        def quantize_weight(raw, engines, calls, name):
+            grouped = keep.tile([P, PACK, P, PACK], BF16, name=name + "_bf", align_bytes=64)
+            codes = keep.tile([P, H], U32, name=name + "_codes", align_bytes=64)
+            scales = keep.tile([P, H], U8, name=name + "_scales", align_bytes=64)
+            m_part = P // len(raw)
+            for h, part in enumerate(raw):
+                dst = grouped[:, :, h * m_part : (h + 1) * m_part, :].rearrange("p t m j -> p m j t")
+                src = part[:].rearrange("p j (m t) -> p m j t", t=PACK)
+                if engines[h] == "S":
+                    nc.scalar.activation(dst, src, COPY)
+                else:
+                    nc.vector.tensor_copy(dst, src)
+            flat = grouped[:].rearrange("p t m j -> p (t m j)")
+            width = H // calls
+            for c in range(calls):
+                nc.vector.quantize_mx(
+                    out=codes[:, c * width : (c + 1) * width].bitcast(FP8X4),
+                    scales=scales[:, c * width : (c + 1) * width],
+                    in_=flat[:, c * width * PACK : (c + 1) * width * PACK],
+                )
+            return codes, scales
+
+        def product_pass(banks, w_q, o):
+            codes, scales = w_q
+            for t in range(PACK):
+                cols = slice(t * P, (t + 1) * P)
+                nc.tensor.matmul_mx(
+                    out=banks[t][:],
+                    lhsT=codes[:, cols].bitcast(FP8X4),
+                    lhsT_scale=scales[:, cols],
+                    rhs=x_codes[o][:].bitcast(FP8X4),
+                    rhs_scale=x_scale[4 * o : P, :],
+                    start=(o == 0),
+                    stop=(o == PASSES - 1),
+                )
+
+        z_banks = [psum.tile([P, S], F32, name="z_bank%d" % t, tag="bank%d" % t) for t in range(PACK)]
+        y_banks = [psum.tile([P, S], F32, name="y_bank%d" % t, tag="bank%d" % (PACK + t)) for t in range(PACK)]
+
+        x_codes = [None] * PASSES
+        x_scale = keep.tile([P, S], U8, name="x_scale", align_bytes=64)
+        nc.vector.tensor_copy(x_scale[:], scale_table[:].indirect(offs_sb[:]))
+        w2_first = quantize_weight(w2_raw[0], "S", 1, "w2_0")
+        x_codes[0] = gather_words(0)
+        product_pass(z_banks, w2_first, 0)
+        w2_last = quantize_weight(w2_raw[1], "V", 1, "w2_1")
+        x_codes[1] = gather_words(1)
+        product_pass(z_banks, w2_last, 1)
+
+        sign = keep.tile([P, PACK], F32, name="sign")
+        step = keep.tile([P, PACK], F32, name="step")
+        size = keep.tile([P, PACK], F32, name="size")
+        nc.vector.tensor_scalar(step[:], unit_sb[:], 0.0, 2.0, ALU.is_ge, ALU.mult)
+        nc.vector.tensor_scalar(sign[:], step[:], -1.0, None, ALU.add)
+        nc.vector.tensor_tensor(size[:], unit_sb[:], sign[:], ALU.mult)
+
+        rate = [keep.tile([P, S], F32, name="rate%d" % t) for t in range(PACK)]
+        value = [keep.tile([P, S], F32, name="value%d" % t) for t in range(PACK)]
+        starts = [sum(CHUNKS[:c]) for c in range(len(CHUNKS))]
+
+        def piece(lst, c):
+            return lst[:, starts[c] // 16 : (starts[c] + CHUNKS[c]) // 16]
+
+        shared = {"right1": "first0", "first2": "spare0", "second2": "left0", "spare2": "right0", "right2": "first1"}
+
+        def quad(name, c):
+            full = "%s%d" % (name, c)
+            return keep.tile([P, PACK, CHUNKS[c]], F32, name=full, tag=shared.get(full, full))
+
+        spare0 = quad("spare", 0)
+        for t in range(PACK):
+            nc.scalar.activation(rate[t][:], z_banks[t][:], COPY, scale=size[:, t : t + 1])
+            nc.scalar.activation(spare0[:, t, :], rate[t][:].indirect(piece(usr_sb, 0)), COPY)
+
+        product_pass(y_banks, quantize_weight(w1_raw[0], "VV", 1, "w1_0"), 0)
+        product_pass(y_banks, quantize_weight(w1_raw[1], "VV", 4, "w1_1"), 1)
+        for t in range(PACK):
+            nc.vector.tensor_tensor(value[t][:], y_banks[t][:], rate[t][:], ALU.mult)
+
+        w3_bf = keep.tile([P, N, PACK], BF16, name="w3_bf", align_bytes=64)
+        w3_codes = keep.tile([P, N], U32, name="w3_codes", align_bytes=64)
+        w3_scales = keep.tile([P, N], U8, name="w3_scales", align_bytes=64)
+        nc.vector.tensor_tensor(
+            w3_bf[:], w3_raw[:].rearrange("p j n -> p n j"), sign[:].unsqueeze(1).to_broadcast([P, N, PACK]), ALU.mult
+        )
+        nc.vector.quantize_mx(
+            out=w3_codes[:].bitcast(FP8X4), scales=w3_scales[:], in_=w3_bf[:].rearrange("p n j -> p (n j)")
+        )
+
+        for c, width in enumerate(CHUNKS):
+            first, second = quad("first", c), quad("second", c)
+            left, right = quad("left", c), quad("right", c)
+            spare = spare0 if c == 0 else quad("spare", c)
+            for t in range(PACK):
+                if t // 2 in FUSED[c]:
+                    nc.scalar.activation(first[:, t, :], value[t][:].indirect(piece(b1_sb, c)), COPY, scale=-1.0)
+                    nc.vector.tensor_tensor(second[:, t, :], value[t][:].indirect(piece(b2_sb, c)), first[:, t, :], ALU.add)
+                else:
+                    nc.scalar.activation(first[:, t, :], value[t][:].indirect(piece(b1_sb, c)), COPY)
+                    nc.scalar.activation(second[:, t, :], value[t][:].indirect(piece(b2_sb, c)), COPY)
+            if c > 0:
+                for t in range(PACK):
+                    user = spare if t // 2 in FUSED[c] else right
+                    nc.scalar.activation(user[:, t, :], rate[t][:].indirect(piece(usr_sb, c)), COPY)
+            for h in range(2):
+                pair = slice(2 * h, 2 * h + 2)
+                a, b = first[:, pair, :], second[:, pair, :]
+                if h in FUSED[c]:
+                    nc.vector.scalar_tensor_tensor(left[:, pair, :], b, -0.6, b, ALU.mult, ALU.max)
+                    nc.vector.scalar_tensor_tensor(right[:, pair, :], a, -0.4, spare[:, pair, :], ALU.mult, ALU.add)
+                else:
+                    nc.vector.scalar_tensor_tensor(left[:, pair, :], b, -0.6, a, ALU.mult, ALU.add)
+                    nc.vector.scalar_tensor_tensor(spare[:, pair, :], a, -0.6, b, ALU.mult, ALU.add)
+            for h in range(2):
+                pair = slice(2 * h, 2 * h + 2)
+                if h not in FUSED[c]:
+                    nc.vector.tensor_tensor(left[:, pair, :], left[:, pair, :], spare[:, pair, :], ALU.max)
+            other = right
+            hid_bf = keep.tile([P, width, PACK], BF16, name="hid_bf%d" % c, align_bytes=64)
+            nc.vector.tensor_tensor(
+                hid_bf[:].rearrange("p (g i) t -> p g t i", i=4),
+                left[:].rearrange("p t (g i) -> p g t i", i=4),
+                other[:].rearrange("p t (g i) -> p g t i", i=4),
+                ALU.add,
+            )
+            hid_codes = keep.tile([P, width], U32, name="hid_codes%d" % c, align_bytes=64)
+            hid_scales = keep.tile([P, width], U8, name="hid_scales%d" % c, align_bytes=64)
+            nc.vector.quantize_mx(
+                out=hid_codes[:].bitcast(FP8X4), scales=hid_scales[:], in_=hid_bf[:].rearrange("p r t -> p (r t)")
+            )
+            acc = psum.tile([N, width], F32, name="acc%d" % c, tag="bank%d" % c)
+            lo = 0
+            while lo < width:
+                n = max(x for x in (512, 256, 128) if x <= width - lo)
+                nc.tensor.matmul_mx(
+                    out=acc[:, lo : lo + n],
+                    lhsT=w3_codes[:].bitcast(FP8X4),
+                    lhsT_scale=w3_scales[:],
+                    rhs=hid_codes[:, lo : lo + n].bitcast(FP8X4),
+                    rhs_scale=hid_scales[:, lo : lo + n],
+                    start=True,
+                    stop=True,
+                )
+                lo += n
+            result = keep.tile([N, width], F32, name="result%d" % c)
+            nc.scalar.activation(result[:], acc[:], COPY)
+            nc.sync.dma_start(out[:, starts[c] : starts[c] + width], result[:])

@@ -20,7 +20,7 @@ PACK = 4
 K_PASS = P * PACK
 PASSES = K // K_PASS
 CHUNKS = (384, 384, 256)
-FUSED = ((0, 1), (), (0,))
+FUSED = ((0, 1, 2, 3), (), (0, 1))
 
 
 def tile_picked_ycompet_sec_p_kernel(tc, x_words, x_scales, w1, w2, unit, w3, offs, b1, b2, usr, out):
@@ -52,14 +52,13 @@ def tile_picked_ycompet_sec_p_kernel(tc, x_words, x_scales, w1, w2, unit, w3, of
 
         scale_table = keep.tile([P, T], U8, name="scale_table")
         nc.vector.memset(scale_table[:].bitcast(I32), 0)
+        x_table = [None] * PASSES
+        w2_raw = [load_weight(w2, 0, 1, "w2")]
         for q in range(4):
-            nc.scalar.dma_start(
+            nc.sync.dma_start(
                 scale_table[32 * q : 32 * q + 4 * PASSES, :].bitcast(I32),
                 x_scales[:, 4 * q : 4 * q + 4, :].bitcast(I32),
             )
-
-        x_table = [None] * PASSES
-        w2_raw = [load_weight(w2, 0, 1, "w2")]
         offs_sb = load_list(offs, "offs_sb")
         x_table[0] = load_words(0)
         w2_raw.append(load_weight(w2, 1, 1, "w2"))
@@ -79,7 +78,7 @@ def tile_picked_ycompet_sec_p_kernel(tc, x_words, x_scales, w1, w2, unit, w3, of
 
         def quantize_weight(raw, engines, calls, name):
             grouped = keep.tile([P, PACK, P, PACK], BF16, name=name + "_bf", align_bytes=64)
-            codes = keep.tile([P, H], U32, name=name + "_codes", align_bytes=64)
+            codes = keep.tile([P, H], U32, name=name + "_codes", tag=name + "_codes", align_bytes=64)
             scales = keep.tile([P, H], U8, name=name + "_scales", align_bytes=64)
             m_part = P // len(raw)
             for h, part in enumerate(raw):
@@ -140,18 +139,15 @@ def tile_picked_ycompet_sec_p_kernel(tc, x_words, x_scales, w1, w2, unit, w3, of
         def piece(lst, c):
             return lst[:, starts[c] // 16 : (starts[c] + CHUNKS[c]) // 16]
 
-        shared = {"right1": "first0", "first2": "spare0", "second2": "left0", "spare2": "right0", "right2": "first1"}
+        def quad(name, width, tag):
+            return keep.tile([P, PACK, width], F32, name=name, tag=tag, align_bytes=64)
 
-        def quad(name, c):
-            full = "%s%d" % (name, c)
-            return keep.tile([P, PACK, CHUNKS[c]], F32, name=full, tag=shared.get(full, full))
-
-        spare0 = quad("spare", 0)
+        product_pass(y_banks, quantize_weight(w1_raw[0], "SV", 1, "w1_0"), 0)
+        user_first = quad("user_first", CHUNKS[0], "user_first")
         for t in range(PACK):
             nc.scalar.activation(rate[t][:], z_banks[t][:], COPY, scale=size[:, t : t + 1])
-            nc.scalar.activation(spare0[:, t, :], rate[t][:].indirect(piece(usr_sb, 0)), COPY)
+            nc.scalar.activation(user_first[:, t, :], rate[t][:].indirect(piece(usr_sb, 0)), COPY)
 
-        product_pass(y_banks, quantize_weight(w1_raw[0], "VV", 1, "w1_0"), 0)
         product_pass(y_banks, quantize_weight(w1_raw[1], "VV", 4, "w1_1"), 1)
         for t in range(PACK):
             nc.vector.tensor_tensor(value[t][:], y_banks[t][:], rate[t][:], ALU.mult)
@@ -166,48 +162,57 @@ def tile_picked_ycompet_sec_p_kernel(tc, x_words, x_scales, w1, w2, unit, w3, of
             out=w3_codes[:].bitcast(FP8X4), scales=w3_scales[:], in_=w3_bf[:].rearrange("p n j -> p (n j)")
         )
 
-        for c, width in enumerate(CHUNKS):
-            first, second = quad("first", c), quad("second", c)
-            left, right = quad("left", c), quad("right", c)
-            spare = spare0 if c == 0 else quad("spare", c)
+        user_rest = quad("user_rest", U - CHUNKS[0], "w1_1_codes")
+
+        chunks = range(len(CHUNKS))
+        first = [quad("first%d" % c, CHUNKS[c], "first%d" % c) for c in chunks]
+        second = [quad("second%d" % c, CHUNKS[c], "second%d" % c) for c in chunks]
+        left = [quad("left%d" % c, CHUNKS[c], "left%d" % c) for c in chunks]
+        spare = [quad("spare%d" % c, CHUNKS[c], "spare%d" % c) for c in chunks]
+        user = [user_first[:]] + [user_rest[:, :, starts[c] - CHUNKS[0] : starts[c] - CHUNKS[0] + CHUNKS[c]] for c in chunks if c > 0]
+
+        def bids(c, t):
+            if t in FUSED[c]:
+                nc.scalar.activation(first[c][:, t, :], value[t][:].indirect(piece(b1_sb, c)), COPY, scale=-1.0)
+                nc.vector.tensor_tensor(second[c][:, t, :], value[t][:].indirect(piece(b2_sb, c)), first[c][:, t, :], ALU.add)
+            else:
+                nc.scalar.activation(first[c][:, t, :], value[t][:].indirect(piece(b1_sb, c)), COPY)
+                nc.scalar.activation(second[c][:, t, :], value[t][:].indirect(piece(b2_sb, c)), COPY)
+
+        def users(c):
             for t in range(PACK):
-                if t // 2 in FUSED[c]:
-                    nc.scalar.activation(first[:, t, :], value[t][:].indirect(piece(b1_sb, c)), COPY, scale=-1.0)
-                    nc.vector.tensor_tensor(second[:, t, :], value[t][:].indirect(piece(b2_sb, c)), first[:, t, :], ALU.add)
-                else:
-                    nc.scalar.activation(first[:, t, :], value[t][:].indirect(piece(b1_sb, c)), COPY)
-                    nc.scalar.activation(second[:, t, :], value[t][:].indirect(piece(b2_sb, c)), COPY)
-            if c > 0:
-                for t in range(PACK):
-                    user = spare if t // 2 in FUSED[c] else right
-                    nc.scalar.activation(user[:, t, :], rate[t][:].indirect(piece(usr_sb, c)), COPY)
-            for h in range(2):
-                pair = slice(2 * h, 2 * h + 2)
-                a, b = first[:, pair, :], second[:, pair, :]
-                if h in FUSED[c]:
-                    nc.vector.scalar_tensor_tensor(left[:, pair, :], b, -0.6, b, ALU.mult, ALU.max)
-                    nc.vector.scalar_tensor_tensor(right[:, pair, :], a, -0.4, spare[:, pair, :], ALU.mult, ALU.add)
-                else:
-                    nc.vector.scalar_tensor_tensor(left[:, pair, :], b, -0.6, a, ALU.mult, ALU.add)
-                    nc.vector.scalar_tensor_tensor(spare[:, pair, :], a, -0.6, b, ALU.mult, ALU.add)
-            for h in range(2):
-                pair = slice(2 * h, 2 * h + 2)
-                if h not in FUSED[c]:
-                    nc.vector.tensor_tensor(left[:, pair, :], left[:, pair, :], spare[:, pair, :], ALU.max)
-            other = right
-            hid_bf = keep.tile([P, width, PACK], BF16, name="hid_bf%d" % c, align_bytes=64)
+                nc.scalar.activation(user[c][:, t, :], rate[t][:].indirect(piece(usr_sb, c)), COPY)
+
+        def compete(c, ts):
+            a, b = first[c][:, ts, :], second[c][:, ts, :]
+            if ts.start in FUSED[c]:
+                nc.vector.scalar_tensor_tensor(left[c][:, ts, :], b, -0.6, b, ALU.mult, ALU.max)
+                nc.vector.scalar_tensor_tensor(user[c][:, ts, :], a, -0.4, user[c][:, ts, :], ALU.mult, ALU.add)
+            else:
+                nc.vector.scalar_tensor_tensor(left[c][:, ts, :], b, -0.6, a, ALU.mult, ALU.add)
+                nc.vector.scalar_tensor_tensor(spare[c][:, ts, :], a, -0.6, b, ALU.mult, ALU.add)
+
+        def larger(c, ts):
+            if ts.start not in FUSED[c]:
+                nc.vector.tensor_tensor(left[c][:, ts, :], left[c][:, ts, :], spare[c][:, ts, :], ALU.max)
+
+        def combine(c, lo, width):
+            hid_bf = keep.tile([P, width, PACK], BF16, name="hid_bf%d_%d" % (c, lo), align_bytes=64)
             nc.vector.tensor_tensor(
                 hid_bf[:].rearrange("p (g i) t -> p g t i", i=4),
-                left[:].rearrange("p t (g i) -> p g t i", i=4),
-                other[:].rearrange("p t (g i) -> p g t i", i=4),
+                left[c][:, :, lo : lo + width].rearrange("p t (g i) -> p g t i", i=4),
+                user[c][:, :, lo : lo + width].rearrange("p t (g i) -> p g t i", i=4),
                 ALU.add,
             )
-            hid_codes = keep.tile([P, width], U32, name="hid_codes%d" % c, align_bytes=64)
-            hid_scales = keep.tile([P, width], U8, name="hid_scales%d" % c, align_bytes=64)
+            return hid_bf
+
+        def markets(hid_bf, start, width, bank):
+            hid_codes = keep.tile([P, width], U32, name="hid_codes%d" % start, align_bytes=64)
+            hid_scales = keep.tile([P, width], U8, name="hid_scales%d" % start, align_bytes=64)
             nc.vector.quantize_mx(
                 out=hid_codes[:].bitcast(FP8X4), scales=hid_scales[:], in_=hid_bf[:].rearrange("p r t -> p (r t)")
             )
-            acc = psum.tile([N, width], F32, name="acc%d" % c, tag="bank%d" % c)
+            acc = psum.tile([N, width], F32, name="acc%d" % start, tag="bank%d" % bank)
             lo = 0
             while lo < width:
                 n = max(x for x in (512, 256, 128) if x <= width - lo)
@@ -221,6 +226,31 @@ def tile_picked_ycompet_sec_p_kernel(tc, x_words, x_scales, w1, w2, unit, w3, of
                     stop=True,
                 )
                 lo += n
-            result = keep.tile([N, width], F32, name="result%d" % c)
+            result = keep.tile([N, width], F32, name="result%d" % start)
             nc.scalar.activation(result[:], acc[:], COPY)
-            nc.sync.dma_start(out[:, starts[c] : starts[c] + width], result[:])
+            nc.sync.dma_start(out[:, start : start + width], result[:])
+
+        def finish(c, parts=1):
+            width = CHUNKS[c] // parts
+            hids = [combine(c, h * width, width) for h in range(parts)]
+            for h in range(parts):
+                markets(hids[h], starts[c] + h * width, width, c + h)
+
+        for t in range(PACK):
+            one = slice(t, t + 1)
+            bids(0, t)
+            bids(1, t)
+            compete(1, one)
+            compete(0, one)
+            larger(1, one)
+        finish(0)
+        users(1)
+        finish(1)
+        for t in range(PACK):
+            bids(2, t)
+        users(2)
+        for h in (1, 0):
+            compete(2, slice(2 * h, 2 * h + 2))
+        for h in range(2):
+            larger(2, slice(2 * h, 2 * h + 2))
+        finish(2, 2)

@@ -20,7 +20,7 @@ PACK = 4
 K_PASS = P * PACK
 PASSES = K // K_PASS
 CHUNKS = (384, 384, 256)
-FUSED = ((0, 1, 2, 3), (), (0, 1))
+EARLY = 3
 
 
 def tile_picked_ycompet_sec_p_kernel(tc, x_words, x_scales, w1, w2, unit, w3, offs, b1, b2, usr, out):
@@ -52,13 +52,17 @@ def tile_picked_ycompet_sec_p_kernel(tc, x_words, x_scales, w1, w2, unit, w3, of
 
         scale_table = keep.tile([P, T], U8, name="scale_table")
         nc.vector.memset(scale_table[:].bitcast(I32), 0)
+
+        def load_scales():
+            for q in range(4):
+                nc.sync.dma_start(
+                    scale_table[32 * q : 32 * q + 4 * PASSES, :].bitcast(I32),
+                    x_scales[:, 4 * q : 4 * q + 4, :].bitcast(I32),
+                )
+
         x_table = [None] * PASSES
         w2_raw = [load_weight(w2, 0, 1, "w2")]
-        for q in range(4):
-            nc.sync.dma_start(
-                scale_table[32 * q : 32 * q + 4 * PASSES, :].bitcast(I32),
-                x_scales[:, 4 * q : 4 * q + 4, :].bitcast(I32),
-            )
+        load_scales()
         offs_sb = load_list(offs, "offs_sb")
         x_table[0] = load_words(0)
         w2_raw.append(load_weight(w2, 1, 1, "w2"))
@@ -79,7 +83,7 @@ def tile_picked_ycompet_sec_p_kernel(tc, x_words, x_scales, w1, w2, unit, w3, of
         def quantize_weight(raw, engines, calls, name):
             grouped = keep.tile([P, PACK, P, PACK], BF16, name=name + "_bf", align_bytes=64)
             codes = keep.tile([P, H], U32, name=name + "_codes", tag=name + "_codes", align_bytes=64)
-            scales = keep.tile([P, H], U8, name=name + "_scales", align_bytes=64)
+            scales = keep.tile([P, H], U8, name=name + "_scales", tag=name + "_scales", align_bytes=64)
             m_part = P // len(raw)
             for h, part in enumerate(raw):
                 dst = grouped[:, :, h * m_part : (h + 1) * m_part, :].rearrange("p t m j -> p m j t")
@@ -142,11 +146,15 @@ def tile_picked_ycompet_sec_p_kernel(tc, x_words, x_scales, w1, w2, unit, w3, of
         def quad(name, width, tag):
             return keep.tile([P, PACK, width], F32, name=name, tag=tag, align_bytes=64)
 
-        product_pass(y_banks, quantize_weight(w1_raw[0], "SV", 1, "w1_0"), 0)
-        user_first = quad("user_first", CHUNKS[0], "user_first")
+        product_pass(y_banks, quantize_weight(w1_raw[0], "VV", 1, "w1_0"), 0)
+        def fetch(dst, window, lst, c, scale=1.0):
+            nc.scalar.activation(dst, window[:].indirect(piece(lst, c)), COPY, scale=scale)
+
+        user_early = keep.tile([P, EARLY, CHUNKS[0]], F32, name="user_early")
         for t in range(PACK):
             nc.scalar.activation(rate[t][:], z_banks[t][:], COPY, scale=size[:, t : t + 1])
-            nc.scalar.activation(user_first[:, t, :], rate[t][:].indirect(piece(usr_sb, 0)), COPY)
+            if t < EARLY:
+                fetch(user_early[:, t, :], rate[t], usr_sb, 0)
 
         product_pass(y_banks, quantize_weight(w1_raw[1], "VV", 4, "w1_1"), 1)
         for t in range(PACK):
@@ -162,52 +170,55 @@ def tile_picked_ycompet_sec_p_kernel(tc, x_words, x_scales, w1, w2, unit, w3, of
             out=w3_codes[:].bitcast(FP8X4), scales=w3_scales[:], in_=w3_bf[:].rearrange("p n j -> p (n j)")
         )
 
-        user_rest = quad("user_rest", U - CHUNKS[0], "w1_1_codes")
-
         chunks = range(len(CHUNKS))
         first = [quad("first%d" % c, CHUNKS[c], "first%d" % c) for c in chunks]
         second = [quad("second%d" % c, CHUNKS[c], "second%d" % c) for c in chunks]
         left = [quad("left%d" % c, CHUNKS[c], "left%d" % c) for c in chunks]
-        spare = [quad("spare%d" % c, CHUNKS[c], "spare%d" % c) for c in chunks]
-        user = [user_first[:]] + [user_rest[:, :, starts[c] - CHUNKS[0] : starts[c] - CHUNKS[0] + CHUNKS[c]] for c in chunks if c > 0]
+        spare = [None] + [quad("spare%d" % c, CHUNKS[c], "spare%d" % c) for c in chunks[1:]]
+        late_shapes = [(PACK, CHUNKS[1]), (PACK, CHUNKS[2]), (PACK - EARLY, CHUNKS[0]), (2, CHUNKS[2])]
+        late = keep.tile([P, sum(r * w for r, w in late_shapes)], F32, name="late", tag="w1_1_codes", align_bytes=64)
+        views = []
+        for i, (r, w) in enumerate(late_shapes):
+            lo = sum(a * b for a, b in late_shapes[:i])
+            views.append(late[:, lo : lo + r * w].rearrange("p (t r) -> p t r", t=r))
+        right = [quad("right0", CHUNKS[0], "right0")[:], views[0], views[1]]
+        user_late, user_last = views[2], views[3]
 
-        def bids(c, t):
-            if t in FUSED[c]:
-                nc.scalar.activation(first[c][:, t, :], value[t][:].indirect(piece(b1_sb, c)), COPY, scale=-1.0)
-                nc.vector.tensor_tensor(second[c][:, t, :], value[t][:].indirect(piece(b2_sb, c)), first[c][:, t, :], ALU.add)
-            else:
-                nc.scalar.activation(first[c][:, t, :], value[t][:].indirect(piece(b1_sb, c)), COPY)
-                nc.scalar.activation(second[c][:, t, :], value[t][:].indirect(piece(b2_sb, c)), COPY)
+        def gap(c, t):
+            fetch(first[c][:, t, :], value[t], b1_sb, c, -1.0)
+            nc.vector.tensor_tensor(second[c][:, t, :], value[t][:].indirect(piece(b2_sb, c)), first[c][:, t, :], ALU.add)
 
-        def users(c):
-            for t in range(PACK):
-                nc.scalar.activation(user[c][:, t, :], rate[t][:].indirect(piece(usr_sb, c)), COPY)
+        def both(c, t):
+            fetch(first[c][:, t, :], value[t], b1_sb, c)
+            fetch(second[c][:, t, :], value[t], b2_sb, c)
 
-        def compete(c, ts):
+        def base(c, ts, user):
+            nc.vector.scalar_tensor_tensor(right[c][:, ts, :], first[c][:, ts, :], -0.4, user, ALU.mult, ALU.add)
+
+        def bend(c, ts):
+            d = second[c][:, ts, :]
+            nc.vector.scalar_tensor_tensor(left[c][:, ts, :], d, -0.6, d, ALU.mult, ALU.max)
+
+        def outcomes(c, ts):
             a, b = first[c][:, ts, :], second[c][:, ts, :]
-            if ts.start in FUSED[c]:
-                nc.vector.scalar_tensor_tensor(left[c][:, ts, :], b, -0.6, b, ALU.mult, ALU.max)
-                nc.vector.scalar_tensor_tensor(user[c][:, ts, :], a, -0.4, user[c][:, ts, :], ALU.mult, ALU.add)
-            else:
-                nc.vector.scalar_tensor_tensor(left[c][:, ts, :], b, -0.6, a, ALU.mult, ALU.add)
-                nc.vector.scalar_tensor_tensor(spare[c][:, ts, :], a, -0.6, b, ALU.mult, ALU.add)
+            nc.vector.scalar_tensor_tensor(left[c][:, ts, :], b, -0.6, a, ALU.mult, ALU.add)
+            nc.vector.scalar_tensor_tensor(spare[c][:, ts, :], a, -0.6, b, ALU.mult, ALU.add)
 
         def larger(c, ts):
-            if ts.start not in FUSED[c]:
-                nc.vector.tensor_tensor(left[c][:, ts, :], left[c][:, ts, :], spare[c][:, ts, :], ALU.max)
+            nc.vector.tensor_tensor(left[c][:, ts, :], left[c][:, ts, :], spare[c][:, ts, :], ALU.max)
 
         def combine(c, lo, width):
             hid_bf = keep.tile([P, width, PACK], BF16, name="hid_bf%d_%d" % (c, lo), align_bytes=64)
             nc.vector.tensor_tensor(
                 hid_bf[:].rearrange("p (g i) t -> p g t i", i=4),
                 left[c][:, :, lo : lo + width].rearrange("p t (g i) -> p g t i", i=4),
-                user[c][:, :, lo : lo + width].rearrange("p t (g i) -> p g t i", i=4),
+                right[c][:, :, lo : lo + width].rearrange("p t (g i) -> p g t i", i=4),
                 ALU.add,
             )
             return hid_bf
 
         def markets(hid_bf, start, width, bank):
-            hid_codes = keep.tile([P, width], U32, name="hid_codes%d" % start, align_bytes=64)
+            hid_codes = keep.tile([P, width], U32, name="hid_codes%d" % start, tag="hid_codes%d" % start, align_bytes=64)
             hid_scales = keep.tile([P, width], U8, name="hid_scales%d" % start, align_bytes=64)
             nc.vector.quantize_mx(
                 out=hid_codes[:].bitcast(FP8X4), scales=hid_scales[:], in_=hid_bf[:].rearrange("p r t -> p (r t)")
@@ -228,29 +239,41 @@ def tile_picked_ycompet_sec_p_kernel(tc, x_words, x_scales, w1, w2, unit, w3, of
                 lo += n
             result = keep.tile([N, width], F32, name="result%d" % start)
             nc.scalar.activation(result[:], acc[:], COPY)
-            nc.sync.dma_start(out[:, start : start + width], result[:])
-
-        def finish(c, parts=1):
-            width = CHUNKS[c] // parts
-            hids = [combine(c, h * width, width) for h in range(parts)]
-            for h in range(parts):
-                markets(hids[h], starts[c] + h * width, width, c + h)
+            queue = nc.scalar if start + width == U else nc.sync
+            queue.dma_start(out[:, start : start + width], result[:])
 
         for t in range(PACK):
             one = slice(t, t + 1)
-            bids(0, t)
-            bids(1, t)
-            compete(1, one)
-            compete(0, one)
-            larger(1, one)
-        finish(0)
-        users(1)
-        finish(1)
+            if t >= EARLY:
+                fetch(user_late[:, t - EARLY, :], rate[t], usr_sb, 0)
+            gap(0, t)
+            if t > 0:
+                larger(1, slice(t - 1, t))
+            base(0, one, user_early[:, one, :] if t < EARLY else user_late[:, t - EARLY : t - EARLY + 1, :])
+            bend(0, one)
+            both(1, t)
+            outcomes(1, one)
+        hid0 = combine(0, 0, CHUNKS[0])
+        larger(1, slice(PACK - 1, PACK))
+        markets(hid0, 0, CHUNKS[0], 0)
         for t in range(PACK):
-            bids(2, t)
-        users(2)
-        for h in (1, 0):
-            compete(2, slice(2 * h, 2 * h + 2))
+            fetch(right[1][:, t, :], rate[t], usr_sb, 1)
+        hid1 = combine(1, 0, CHUNKS[1])
+        low, high = slice(0, 2), slice(2, 4)
+        gap(2, 0)
+        markets(hid1, starts[1], CHUNKS[1], 1)
+        gap(2, 1)
+        for t in (2, 3):
+            both(2, t)
+        for t in (0, 1):
+            fetch(user_last[:, t, :], rate[t], usr_sb, 2)
+        for t in (2, 3):
+            fetch(right[2][:, t, :], rate[t], usr_sb, 2)
+        outcomes(2, high)
+        bend(2, low)
+        larger(2, high)
+        base(2, low, user_last)
+        half = CHUNKS[2] // 2
+        hids = [combine(2, h * half, half) for h in range(2)]
         for h in range(2):
-            larger(2, slice(2 * h, 2 * h + 2))
-        finish(2, 2)
+            markets(hids[h], starts[2] + h * half, half, 2 + h)

from contextlib import ExitStack

import concourse.mybir as mybir

K, T, S, N, H, U = 1024, 2048, 512, 128, 512, 1024
FLOPS = 2 * (2 * K * H * S + H * N * U)

F32 = mybir.dt.float32
BF16 = mybir.dt.bfloat16
I32 = mybir.dt.int32
U32 = mybir.dt.uint32
U16 = mybir.dt.uint16
U8 = mybir.dt.uint8
FP8X4 = mybir.dt.float8_e4m3fn_x4
ALU = mybir.AluOpType
COPY = mybir.ActivationFunctionType.Copy

P = 128
PACK = 4
K_PASS = P * PACK
PASSES = K // K_PASS
CHUNKS = (384, 384, 256)
EARLY = 3


def tile_picked_ycompet_sec_p_kernel(tc, x_words, x_scales, w1, w2, unit, w3, offs, b1, b2, usr, out):
    nc = tc.nc
    with ExitStack() as ctx:
        lists = ctx.enter_context(tc.tile_pool(name="lists", bufs=1))
        keep = ctx.enter_context(tc.tile_pool(name="keep", bufs=1))
        psum = ctx.enter_context(tc.psum_pool(name="psum", bufs=1))

        def load_list(src, name):
            tile = lists.tile(list(src.shape), U16, name=name)
            nc.sync.dma_start(tile[:], src)
            return tile

        def load_words(o):
            tile = keep.tile([P, T], I32, name="x_table%d" % o)
            nc.sync.dma_start(tile[:], x_words[o].rearrange("p n r -> p (n r)").bitcast(I32))
            return tile

        def load_weight(w, o, parts, name):
            width = w.shape[1] // parts
            tiles = []
            for h in range(parts):
                tile = keep.tile([P, PACK, width], F32, name="%s_raw%d_%d" % (name, o, h))
                rows = w[o * K_PASS : (o + 1) * K_PASS, h * width : (h + 1) * width]
                nc.sync.dma_start(tile[:], rows.rearrange("(p j) c -> p j c", j=PACK))
                tiles.append(tile)
            return tiles

        scale_table = keep.tile([P, T], U8, name="scale_table")
        nc.vector.memset(scale_table[:].bitcast(I32), 0)

        def load_scales():
            for q in range(4):
                nc.sync.dma_start(
                    scale_table[32 * q : 32 * q + 4 * PASSES, :].bitcast(I32),
                    x_scales[:, 4 * q : 4 * q + 4, :].bitcast(I32),
                )

        x_table = [None] * PASSES
        w2_raw = [load_weight(w2, 0, 1, "w2")]
        load_scales()
        offs_sb = load_list(offs, "offs_sb")
        x_table[0] = load_words(0)
        w2_raw.append(load_weight(w2, 1, 1, "w2"))
        x_table[1] = load_words(1)
        unit_sb = keep.tile([P, PACK], F32, name="unit_sb")
        nc.sync.dma_start(unit_sb[:], unit.rearrange("(p t) one -> p (t one)", t=PACK))
        usr_sb = load_list(usr, "usr_sb")
        w1_raw = [load_weight(w1, 0, 2, "w1"), load_weight(w1, 1, 2, "w1")]
        b1_sb = load_list(b1, "b1_sb")
        b2_sb = load_list(b2, "b2_sb")
        w3_raw = load_weight(w3, 0, 1, "w3")[0]

        def gather_words(o):
            tile = keep.tile([P, S], U32, name="x_codes%d" % o, align_bytes=64)
            nc.vector.tensor_copy(tile[:], x_table[o][:].bitcast(U32).indirect(offs_sb[:]))
            return tile

        def quantize_weight(raw, engines, calls, name):
            grouped = keep.tile([P, PACK, P, PACK], BF16, name=name + "_bf", align_bytes=64)
            codes = keep.tile([P, H], U32, name=name + "_codes", tag=name + "_codes", align_bytes=64)
            scales = keep.tile([P, H], U8, name=name + "_scales", tag=name + "_scales", align_bytes=64)
            m_part = P // len(raw)
            for h, part in enumerate(raw):
                dst = grouped[:, :, h * m_part : (h + 1) * m_part, :].rearrange("p t m j -> p m j t")
                src = part[:].rearrange("p j (m t) -> p m j t", t=PACK)
                if engines[h] == "S":
                    nc.scalar.activation(dst, src, COPY)
                else:
                    nc.vector.tensor_copy(dst, src)
            flat = grouped[:].rearrange("p t m j -> p (t m j)")
            width = H // calls
            for c in range(calls):
                nc.vector.quantize_mx(
                    out=codes[:, c * width : (c + 1) * width].bitcast(FP8X4),
                    scales=scales[:, c * width : (c + 1) * width],
                    in_=flat[:, c * width * PACK : (c + 1) * width * PACK],
                )
            return codes, scales

        def product_pass(banks, w_q, o):
            codes, scales = w_q
            for t in range(PACK):
                cols = slice(t * P, (t + 1) * P)
                nc.tensor.matmul_mx(
                    out=banks[t][:],
                    lhsT=codes[:, cols].bitcast(FP8X4),
                    lhsT_scale=scales[:, cols],
                    rhs=x_codes[o][:].bitcast(FP8X4),
                    rhs_scale=x_scale[4 * o : P, :],
                    start=(o == 0),
                    stop=(o == PASSES - 1),
                )

        z_banks = [psum.tile([P, S], F32, name="z_bank%d" % t, tag="bank%d" % t) for t in range(PACK)]
        y_banks = [psum.tile([P, S], F32, name="y_bank%d" % t, tag="bank%d" % (PACK + t)) for t in range(PACK)]

        x_codes = [None] * PASSES
        x_scale = keep.tile([P, S], U8, name="x_scale", align_bytes=64)
        nc.vector.tensor_copy(x_scale[:], scale_table[:].indirect(offs_sb[:]))
        w2_first = quantize_weight(w2_raw[0], "S", 1, "w2_0")
        x_codes[0] = gather_words(0)
        product_pass(z_banks, w2_first, 0)
        w2_last = quantize_weight(w2_raw[1], "V", 1, "w2_1")
        x_codes[1] = gather_words(1)
        product_pass(z_banks, w2_last, 1)

        sign = keep.tile([P, PACK], F32, name="sign")
        step = keep.tile([P, PACK], F32, name="step")
        size = keep.tile([P, PACK], F32, name="size")
        nc.vector.tensor_scalar(step[:], unit_sb[:], 0.0, 2.0, ALU.is_ge, ALU.mult)
        nc.vector.tensor_scalar(sign[:], step[:], -1.0, None, ALU.add)
        nc.vector.tensor_tensor(size[:], unit_sb[:], sign[:], ALU.mult)

        rate = [keep.tile([P, S], F32, name="rate%d" % t) for t in range(PACK)]
        value = [keep.tile([P, S], F32, name="value%d" % t) for t in range(PACK)]
        starts = [sum(CHUNKS[:c]) for c in range(len(CHUNKS))]

        def piece(lst, c):
            return lst[:, starts[c] // 16 : (starts[c] + CHUNKS[c]) // 16]

        def quad(name, width, tag):
            return keep.tile([P, PACK, width], F32, name=name, tag=tag, align_bytes=64)

        product_pass(y_banks, quantize_weight(w1_raw[0], "VV", 1, "w1_0"), 0)
        def fetch(dst, window, lst, c, scale=1.0):
            nc.scalar.activation(dst, window[:].indirect(piece(lst, c)), COPY, scale=scale)

        user_early = keep.tile([P, EARLY, CHUNKS[0]], F32, name="user_early")
        for t in range(PACK):
            nc.scalar.activation(rate[t][:], z_banks[t][:], COPY, scale=size[:, t : t + 1])
            if t < EARLY:
                fetch(user_early[:, t, :], rate[t], usr_sb, 0)

        product_pass(y_banks, quantize_weight(w1_raw[1], "VV", 4, "w1_1"), 1)
        for t in range(PACK):
            nc.vector.tensor_tensor(value[t][:], y_banks[t][:], rate[t][:], ALU.mult)

        w3_bf = keep.tile([P, N, PACK], BF16, name="w3_bf", align_bytes=64)
        w3_codes = keep.tile([P, N], U32, name="w3_codes", align_bytes=64)
        w3_scales = keep.tile([P, N], U8, name="w3_scales", align_bytes=64)
        nc.vector.tensor_tensor(
            w3_bf[:], w3_raw[:].rearrange("p j n -> p n j"), sign[:].unsqueeze(1).to_broadcast([P, N, PACK]), ALU.mult
        )
        nc.vector.quantize_mx(
            out=w3_codes[:].bitcast(FP8X4), scales=w3_scales[:], in_=w3_bf[:].rearrange("p n j -> p (n j)")
        )

        chunks = range(len(CHUNKS))
        first = [quad("first%d" % c, CHUNKS[c], "first%d" % c) for c in chunks]
        second = [quad("second%d" % c, CHUNKS[c], "second%d" % c) for c in chunks]
        left = [quad("left%d" % c, CHUNKS[c], "left%d" % c) for c in chunks]
        spare = [None] + [quad("spare%d" % c, CHUNKS[c], "spare%d" % c) for c in chunks[1:]]
        late_shapes = [(PACK, CHUNKS[1]), (PACK, CHUNKS[2]), (PACK - EARLY, CHUNKS[0]), (2, CHUNKS[2])]
        late = keep.tile([P, sum(r * w for r, w in late_shapes)], F32, name="late", tag="w1_1_codes", align_bytes=64)
        views = []
        for i, (r, w) in enumerate(late_shapes):
            lo = sum(a * b for a, b in late_shapes[:i])
            views.append(late[:, lo : lo + r * w].rearrange("p (t r) -> p t r", t=r))
        right = [quad("right0", CHUNKS[0], "right0")[:], views[0], views[1]]
        user_late, user_last = views[2], views[3]

        def gap(c, t):
            fetch(first[c][:, t, :], value[t], b1_sb, c, -1.0)
            nc.vector.tensor_tensor(second[c][:, t, :], value[t][:].indirect(piece(b2_sb, c)), first[c][:, t, :], ALU.add)

        def both(c, t):
            fetch(first[c][:, t, :], value[t], b1_sb, c)
            fetch(second[c][:, t, :], value[t], b2_sb, c)

        def base(c, ts, user):
            nc.vector.scalar_tensor_tensor(right[c][:, ts, :], first[c][:, ts, :], -0.4, user, ALU.mult, ALU.add)

        def bend(c, ts):
            d = second[c][:, ts, :]
            nc.vector.scalar_tensor_tensor(left[c][:, ts, :], d, -0.6, d, ALU.mult, ALU.max)

        def outcomes(c, ts):
            a, b = first[c][:, ts, :], second[c][:, ts, :]
            nc.vector.scalar_tensor_tensor(left[c][:, ts, :], b, -0.6, a, ALU.mult, ALU.add)
            nc.vector.scalar_tensor_tensor(spare[c][:, ts, :], a, -0.6, b, ALU.mult, ALU.add)

        def larger(c, ts):
            nc.vector.tensor_tensor(left[c][:, ts, :], left[c][:, ts, :], spare[c][:, ts, :], ALU.max)

        def combine(c, lo, width):
            hid_bf = keep.tile([P, width, PACK], BF16, name="hid_bf%d_%d" % (c, lo), align_bytes=64)
            nc.vector.tensor_tensor(
                hid_bf[:].rearrange("p (g i) t -> p g t i", i=4),
                left[c][:, :, lo : lo + width].rearrange("p t (g i) -> p g t i", i=4),
                right[c][:, :, lo : lo + width].rearrange("p t (g i) -> p g t i", i=4),
                ALU.add,
            )
            return hid_bf

        def markets(hid_bf, start, width, bank):
            hid_codes = keep.tile([P, width], U32, name="hid_codes%d" % start, tag="hid_codes%d" % start, align_bytes=64)
            hid_scales = keep.tile([P, width], U8, name="hid_scales%d" % start, align_bytes=64)
            nc.vector.quantize_mx(
                out=hid_codes[:].bitcast(FP8X4), scales=hid_scales[:], in_=hid_bf[:].rearrange("p r t -> p (r t)")
            )
            acc = psum.tile([N, width], F32, name="acc%d" % start, tag="bank%d" % bank)
            lo = 0
            while lo < width:
                n = max(x for x in (512, 256, 128) if x <= width - lo)
                nc.tensor.matmul_mx(
                    out=acc[:, lo : lo + n],
                    lhsT=w3_codes[:].bitcast(FP8X4),
                    lhsT_scale=w3_scales[:],
                    rhs=hid_codes[:, lo : lo + n].bitcast(FP8X4),
                    rhs_scale=hid_scales[:, lo : lo + n],
                    start=True,
                    stop=True,
                )
                lo += n
            result = keep.tile([N, width], F32, name="result%d" % start)
            nc.scalar.activation(result[:], acc[:], COPY)
            queue = nc.scalar if start + width == U else nc.sync
            queue.dma_start(out[:, start : start + width], result[:])

        for t in range(PACK):
            one = slice(t, t + 1)
            if t >= EARLY:
                fetch(user_late[:, t - EARLY, :], rate[t], usr_sb, 0)
            gap(0, t)
            if t > 0:
                larger(1, slice(t - 1, t))
            base(0, one, user_early[:, one, :] if t < EARLY else user_late[:, t - EARLY : t - EARLY + 1, :])
            bend(0, one)
            both(1, t)
            outcomes(1, one)
        hid0 = combine(0, 0, CHUNKS[0])
        larger(1, slice(PACK - 1, PACK))
        markets(hid0, 0, CHUNKS[0], 0)
        for t in range(PACK):
            fetch(right[1][:, t, :], rate[t], usr_sb, 1)
        hid1 = combine(1, 0, CHUNKS[1])
        low, high = slice(0, 2), slice(2, 4)
        gap(2, 0)
        markets(hid1, starts[1], CHUNKS[1], 1)
        gap(2, 1)
        for t in (2, 3):
            both(2, t)
        for t in (0, 1):
            fetch(user_last[:, t, :], rate[t], usr_sb, 2)
        for t in (2, 3):
            fetch(right[2][:, t, :], rate[t], usr_sb, 2)
        outcomes(2, high)
        bend(2, low)
        larger(2, high)
        base(2, low, user_last)
        half = CHUNKS[2] // 2
        hids = [combine(2, h * half, half) for h in range(2)]
        for h in range(2):
            markets(hids[h], starts[2] + h * half, half, 2 + h)
